import numpy as np
import ml_dtypes


def mxq(x, axis, fmt="e4m3"):
    dtype, down = {"e4m3": (ml_dtypes.float8_e4m3fn, 7), "e5m2": (ml_dtypes.float8_e5m2, 14)}[fmt]
    v = np.moveaxis(np.asarray(x, np.float32).astype(ml_dtypes.bfloat16).astype(np.float64), axis, -1)
    blocks = v.reshape(v.shape[:-1] + (-1, 32))
    amax = np.abs(blocks).max(-1, keepdims=True)
    byte = np.maximum(np.where(amax > 0, np.frexp(amax)[1] - 1 + 127, 0) - down, 1)
    scale = np.exp2(byte - 127.0)
    codes = (blocks / scale).astype(np.float32).astype(dtype).astype(np.float64)
    return np.moveaxis((codes * scale).reshape(v.shape), -1, axis)


WIDE = False


def mx_kscale(k):
    if not WIDE:
        return np.ones(k)
    levels = np.array([10, -10, 5, -5, 0])
    if k % 512:
        return np.exp2(np.random.permutation(np.resize(levels, k // 32))).repeat(32)
    a = np.empty((k // 512, 16))
    for p in range(k // 512):
        a[p, :8] = np.random.permutation(np.resize(levels, 8))
        for g in range(8):
            far = levels[np.abs(levels - a[p, g]) >= 10]
            a[p, g + 8] = far[np.random.randint(len(far))]
    return np.exp2(a.ravel()).repeat(32)


def f64(x):
    return np.asarray(x).astype(np.float64)


def striped(idx):
    return np.tile(np.asarray(idx).reshape(-1, 16).T, (8, 1)).astype(np.uint16)


def unstriped(offs):
    return offs[:16].T.reshape(-1).astype(np.int64)


E2M1 = np.array([0.0, 0.5, 1.0, 1.5, 2.0, 3.0, 4.0, 6.0, -0.0, -0.5, -1.0, -1.5, -2.0, -3.0, -4.0, -6.0])


def pack_weight(w, fmt):
    k, n = w.shape
    w = f64(np.asarray(w, np.float32).astype(ml_dtypes.bfloat16)).reshape(k // 32, 32, n)
    amax = np.abs(w).max(1)
    if fmt == "e4m3":
        byte = np.frexp(amax)[1] - 1 + 127 - 7
    else:
        mant, ex = np.frexp(amax / 6.0)
        byte = np.where(mant > 0.5, ex, ex - 1) + 127
    byte = np.clip(np.where(amax > 0, byte, 1), 1, 254)
    scaled = (w * np.exp2(127.0 - byte)[:, None, :]).reshape(k, n).astype(np.float32)
    by_word = np.ascontiguousarray(scaled.reshape(k // 512, 128, 4, n).transpose(0, 1, 3, 2))
    if fmt == "e4m3":
        words = by_word.astype(ml_dtypes.float8_e4m3fn).view(np.uint8)
    else:
        c = by_word.astype(ml_dtypes.float4_e2m1fn).view(np.uint8) & 0xF
        words = (c[..., 0::2] | (c[..., 1::2] << 4)).reshape(k // 512, 128, 2 * n)
    return np.ascontiguousarray(words), np.ascontiguousarray(byte.astype(np.uint8).reshape(k // 512, 16, n))


def unpack_weight(words, scales, fmt):
    g, _, n = scales.shape
    words = np.ascontiguousarray(words).reshape(g, 128, n, -1)
    if fmt == "e4m3":
        vals = words.view(ml_dtypes.float8_e4m3fn).astype(np.float64)
    else:
        nib = np.empty((g, 128, n, 4), np.uint8)
        nib[..., 0::2] = words & 0xF
        nib[..., 1::2] = words >> 4
        vals = E2M1[nib]
    vals = vals * np.repeat(np.exp2(scales.astype(np.float64) - 127.0), 8, axis=1)[..., None]
    return vals.transpose(0, 1, 3, 2).reshape(g * 512, n)


K, T, J, N = 512, 512, 512, 512


def setup_inputs():
    n = np.random.standard_normal
    idx = np.random.randint(0, T, J)
    idx2 = np.random.randint(0, T, J)
    fk = mx_kscale(K)
    xtp = pack_weight(n((K, T)) / fk[:, None], "e4m3")
    wap = pack_weight(n((K, N)) * 1 / np.sqrt(K) * fk[:, None], "e2m1")
    return {
        "xt_words": xtp[0],
        "xt_scales": xtp[1],
        "wa_words": wap[0],
        "wa_scales": wap[1],
        "wb": (n((K, N)) * 1 / np.sqrt(K) * fk[:, None]).astype(np.float32),
        "sh": (np.random.uniform(0.1, 0.4, (N, 1))).astype(np.float32),
        "offs": striped(idx),
        "offs2": striped(idx2),
    }


def reference(xt_words, xt_scales, wa_words, wa_scales, wb, sh, offs, offs2):
    idx = unstriped(offs)
    idx2 = unstriped(offs2)
    xtu = unpack_weight(xt_words, xt_scales, "e4m3")
    wau = unpack_weight(wa_words, wa_scales, "e2m1")
    z = wau.T @ xtu
    wbq = mxq(f64(wb), 0, "e4m3")
    u = wbq.T @ xtu
    y = z[:, idx] / (1.0 + np.maximum(u[:, idx2], 0.0)) + f64(sh) * u[:, idx]
    return y

@@ -1,0 +1,142 @@
+from contextlib import ExitStack
+
+import concourse.mybir as mybir
+
+K, T, J, N = 512, 512, 512, 512
+FLOPS = 2 * 2 * K * T * N
+
+F32 = mybir.dt.float32
+BF16 = mybir.dt.bfloat16
+I32 = mybir.dt.int32
+U32 = mybir.dt.uint32
+U16 = mybir.dt.uint16
+U8 = mybir.dt.uint8
+FP8X4 = mybir.dt.float8_e4m3fn_x4
+FP4X4 = mybir.dt.float4_e2m1fn_x4
+ACT = mybir.ActivationFunctionType
+ALU = mybir.AluOpType
+
+P = 128
+PACK = 4
+TILES = N // P
+U_WINDOW = 704
+Z_WINDOW = 520
+
+
+def tile_list_divided_by_neighbour_kernel(tc, xt_words, xt_scales, wa_words, wa_scales, wb, sh, offs, offs2, out):
+    nc = tc.nc
+    with ExitStack() as ctx:
+        keep = ctx.enter_context(tc.tile_pool(name="keep", bufs=1))
+        psum = ctx.enter_context(tc.psum_pool(name="psum", bufs=1))
+
+        own = keep.tile([P, J // 16], U16, name="own")
+        nbr = keep.tile([P, J // 16], U16, name="nbr")
+        xt_codes = keep.tile([P, T], U32, name="xt_codes", align_bytes=64)
+        xt_plane = keep.tile([P, T], U8, name="xt_plane", align_bytes=64)
+        wa_codes = keep.tile([P, 2 * N], U8, name="wa_codes", align_bytes=64)
+        wa_plane = keep.tile([P, N], U8, name="wa_plane", align_bytes=64)
+        share = keep.tile([P, TILES], F32, name="share")
+        warm = keep.tile([P, 1], F32, name="warm")
+        warm_out = keep.tile([P, 1], F32, name="warm_out")
+
+        def tiles(name, shape, dtype):
+            return [keep.tile(shape, dtype, name="%s%d" % (name, i), align_bytes=64) for i in range(TILES)]
+
+        wb_raw = tiles("wb_raw", [P, PACK, P], F32)
+        wb_grouped = tiles("wb_grouped", [P, P, PACK], BF16)
+        wb_codes = tiles("wb_codes", [P, P], U32)
+        wb_plane = tiles("wb_plane", [P, P], U8)
+        u = tiles("u", [P, U_WINDOW], F32)
+        z = tiles("z", [P, Z_WINDOW], F32)
+        u_nbr = tiles("u_nbr", [P, J], F32)
+        drive = tiles("drive", [P, J], F32)
+        root = tiles("root", [P, J], F32)
+        inv = tiles("inv", [P, J], F32)
+        u_own = tiles("u_own", [P, J], F32)
+        quot = tiles("quot", [P, J], F32)
+        res = tiles("res", [P, J], F32)
+        u_acc = [psum.tile([P, T], F32, name="u_acc%d" % i) for i in range(TILES)]
+        z_acc = [psum.tile([P, T], F32, name="z_acc%d" % i) for i in range(TILES)]
+
+        nc.gpsimd.memset(warm[:], 1.0)
+        nc.scalar.activation(warm_out[:], warm[:], ACT.Abs_reciprocal_sqrt)
+
+        def load_wb(i):
+            nc.sync.dma_start(wb_raw[i][:], wb[:, i * P : (i + 1) * P].rearrange("(p t) n -> p t n", t=PACK))
+
+        def load_plane(plane, rows):
+            for q in range(4):
+                nc.sync.dma_start(plane[32 * q : 32 * q + 4, :].bitcast(I32), rows[0, 4 * q : 4 * q + 4, :].bitcast(I32))
+
+        load_wb(0)
+        load_plane(xt_plane, xt_scales)
+        nc.sync.dma_start(xt_codes[:].bitcast(I32), xt_words[0].rearrange("p c r -> p (c r)").bitcast(I32))
+        load_wb(1)
+        nc.sync.dma_start(nbr[:], offs2)
+        load_wb(2)
+        load_wb(3)
+        nc.sync.dma_start(own[:], offs)
+        nc.sync.dma_start(wa_codes[:].bitcast(I32), wa_words[0].bitcast(I32))
+        load_plane(wa_plane, wa_scales)
+        with nc.allow_non_contiguous_dma(reason="one share to a partition"):
+            nc.gpsimd.dma_start(share[:], sh.rearrange("(i p) o -> p (i o)", p=P))
+
+        for i in range(TILES):
+            src = wb_raw[i][:].rearrange("p t n -> p n t")
+            if i == 1:
+                nc.scalar.copy(wb_grouped[i][:], src)
+            else:
+                nc.vector.tensor_copy(wb_grouped[i][:], src)
+            nc.vector.quantize_mx(
+                out=wb_codes[i][:].bitcast(FP8X4), scales=wb_plane[i][:], in_=wb_grouped[i][:].rearrange("p n t -> p (n t)")
+            )
+            nc.tensor.matmul_mx(
+                out=u_acc[i][:], lhsT=wb_codes[i][:].bitcast(FP8X4), lhsT_scale=wb_plane[i][:],
+                rhs=xt_codes[:].bitcast(FP8X4), rhs_scale=xt_plane[:], start=True, stop=True,
+            )
+            nc.scalar.copy(u[i][:, :T], u_acc[i][:])
+
+        def pick_nbr(i):
+            nc.vector.tensor_copy(u_nbr[i][:], u[i][:].indirect(nbr[:]))
+            nc.scalar.activation(drive[i][:], u_nbr[i][:], ACT.Relu)
+            nc.scalar.activation(root[i][:], drive[i][:], ACT.Abs_reciprocal_sqrt, bias=1.0)
+            nc.scalar.activation(inv[i][:], root[i][:], ACT.Square)
+
+        def make_z(i):
+            nc.tensor.matmul_mx(
+                out=z_acc[i][:], lhsT=wa_codes[:, 2 * P * i : 2 * P * (i + 1)].bitcast(FP4X4),
+                lhsT_scale=wa_plane[:, P * i : P * (i + 1)],
+                rhs=xt_codes[:].bitcast(FP8X4), rhs_scale=xt_plane[:], start=True, stop=True,
+            )
+            nc.scalar.copy(z[i][:, :T], z_acc[i][:])
+
+        def pick_own(i):
+            nc.vector.tensor_copy(u_own[i][:], u[i][:].indirect(own[:]))
+
+        def divide(i):
+            nc.vector.tensor_tensor(quot[i][:], z[i][:].indirect(own[:]), inv[i][:], ALU.mult)
+
+        def finish(i):
+            nc.vector.scalar_tensor_tensor(res[i][:], u_own[i][:], share[:, i : i + 1], quot[i][:], ALU.mult, ALU.add)
+            nc.sync.dma_start(out[i * P : (i + 1) * P, :], res[i][:])
+
+        pick_nbr(0)
+        make_z(0)
+        pick_nbr(1)
+        make_z(1)
+        pick_own(0)
+        divide(0)
+        pick_nbr(2)
+        make_z(2)
+        finish(0)
+        pick_own(1)
+        divide(1)
+        pick_nbr(3)
+        make_z(3)
+        finish(1)
+        pick_own(2)
+        divide(2)
+        pick_own(3)
+        finish(2)
+        divide(3)
+        finish(3)

@@ -20,14 +20,14 @@ P = 128
 PACK = 4
 TILES = N // P
 U_WINDOW = 704
-Z_WINDOW = 520
+Z_WINDOW = 704
 
 
 def tile_list_divided_by_neighbour_kernel(tc, xt_words, xt_scales, wa_words, wa_scales, wb, sh, offs, offs2, out):
     nc = tc.nc
     with ExitStack() as ctx:
         keep = ctx.enter_context(tc.tile_pool(name="keep", bufs=1))
-        psum = ctx.enter_context(tc.psum_pool(name="psum", bufs=1))
+        psum = ctx.enter_context(tc.psum_pool(name="psum", bufs=8))
 
         own = keep.tile([P, J // 16], U16, name="own")
         nbr = keep.tile([P, J // 16], U16, name="nbr")
@@ -39,30 +39,36 @@ def tile_list_divided_by_neighbour_kernel(tc, xt_words, xt_scales, wa_words, wa_
         warm = keep.tile([P, 1], F32, name="warm")
         warm_out = keep.tile([P, 1], F32, name="warm_out")
 
-        def tiles(name, shape, dtype):
-            return [keep.tile(shape, dtype, name="%s%d" % (name, i), align_bytes=64) for i in range(TILES)]
+        chunks = [slice(0, P), slice(P, 2 * P), slice(2 * P, 4 * P)]
+        wb_raw = [keep.tile([P, PACK, c.stop - c.start], F32, name="wb_raw%d" % c.start, tag="f" if c.start == 2 * P else "wb_raw%d" % c.start, align_bytes=64) for c in chunks]
+        wb_grouped = [
+            keep.tile([P, P, PACK], BF16, name="wb_grouped%d" % i, tag="h" if i == 3 else "wb_grouped%d" % i, align_bytes=64)
+            for i in range(TILES)
+        ]
+        wb_codes = keep.tile([P, N], U32, name="wb_codes", align_bytes=64)
+        wb_plane = keep.tile([P, N], U8, name="wb_plane", align_bytes=64)
+        shared = {
+            "u_nbr0": "a", "u_own0": "a", "u_own1": "a", "u_own2": "a",
+            "root0": "b", "z_own1": "b", "z_own3": "b", "root1": "c", "z_own2": "c",
+            "u_nbr2": "d", "part1": "d", "u_nbr3": "e", "u_own3": "e",
+            "drive0": "f", "drive1": "f", "drive2": "f", "drive3": "f",
+            "u_nbr1": "g", "part0": "g", "z_own0": "h",
+        }
+        made = {}
 
-        wb_raw = tiles("wb_raw", [P, PACK, P], F32)
-        wb_grouped = tiles("wb_grouped", [P, P, PACK], BF16)
-        wb_codes = tiles("wb_codes", [P, P], U32)
-        wb_plane = tiles("wb_plane", [P, P], U8)
-        u = tiles("u", [P, U_WINDOW], F32)
-        z = tiles("z", [P, Z_WINDOW], F32)
-        u_nbr = tiles("u_nbr", [P, J], F32)
-        drive = tiles("drive", [P, J], F32)
-        root = tiles("root", [P, J], F32)
-        inv = tiles("inv", [P, J], F32)
-        u_own = tiles("u_own", [P, J], F32)
-        quot = tiles("quot", [P, J], F32)
-        res = tiles("res", [P, J], F32)
-        u_acc = [psum.tile([P, T], F32, name="u_acc%d" % i) for i in range(TILES)]
-        z_acc = [psum.tile([P, T], F32, name="z_acc%d" % i) for i in range(TILES)]
+        def new(name, i, width):
+            key = "%s%d" % (name, i)
+            made[key] = keep.tile([P, width], F32, name=key, tag=shared.get(key, key), align_bytes=64)
+            return made[key]
+
+        def get(name, i):
+            return made["%s%d" % (name, i)]
 
         nc.gpsimd.memset(warm[:], 1.0)
         nc.scalar.activation(warm_out[:], warm[:], ACT.Abs_reciprocal_sqrt)
 
         def load_wb(i):
-            nc.sync.dma_start(wb_raw[i][:], wb[:, i * P : (i + 1) * P].rearrange("(p t) n -> p t n", t=PACK))
+            nc.sync.dma_start(wb_raw[i][:], wb[:, chunks[i]].rearrange("(p t) n -> p t n", t=PACK))
 
         def load_plane(plane, rows):
             for q in range(4):
@@ -73,70 +79,117 @@ def tile_list_divided_by_neighbour_kernel(tc, xt_words, xt_scales, wa_words, wa_
         nc.sync.dma_start(xt_codes[:].bitcast(I32), xt_words[0].rearrange("p c r -> p (c r)").bitcast(I32))
         load_wb(1)
         nc.sync.dma_start(nbr[:], offs2)
-        load_wb(2)
-        load_wb(3)
-        nc.sync.dma_start(own[:], offs)
         nc.sync.dma_start(wa_codes[:].bitcast(I32), wa_words[0].bitcast(I32))
         load_plane(wa_plane, wa_scales)
+        load_wb(2)
+        nc.sync.dma_start(own[:], offs)
         with nc.allow_non_contiguous_dma(reason="one share to a partition"):
-            nc.gpsimd.dma_start(share[:], sh.rearrange("(i p) o -> p (i o)", p=P))
+            nc.sync.dma_start(share[:], sh.rearrange("(i p) o -> p (i o)", p=P))
 
+        sources = [wb_raw[0][:], wb_raw[1][:], wb_raw[2][:, :, :P], wb_raw[2][:, :, P:]]
         for i in range(TILES):
-            src = wb_raw[i][:].rearrange("p t n -> p n t")
-            if i == 1:
-                nc.scalar.copy(wb_grouped[i][:], src)
+            src = sources[i].rearrange("p t n -> p n t")
+            cols = slice(i * P, (i + 1) * P)
+            if i >= 2:
+                nc.gpsimd.tensor_scalar(wb_grouped[i][:], src, 1.0, 0.0, ALU.mult, ALU.add)
             else:
                 nc.vector.tensor_copy(wb_grouped[i][:], src)
             nc.vector.quantize_mx(
-                out=wb_codes[i][:].bitcast(FP8X4), scales=wb_plane[i][:], in_=wb_grouped[i][:].rearrange("p n t -> p (n t)")
+                out=wb_codes[:, cols].bitcast(FP8X4), scales=wb_plane[:, cols], in_=wb_grouped[i][:].rearrange("p n t -> p (n t)")
             )
+
+        def make_u(i):
+            acc = psum.tile([P, T], F32, name="acc")
             nc.tensor.matmul_mx(
-                out=u_acc[i][:], lhsT=wb_codes[i][:].bitcast(FP8X4), lhsT_scale=wb_plane[i][:],
+                out=acc[:], lhsT=wb_codes[:, P * i : P * (i + 1)].bitcast(FP8X4), lhsT_scale=wb_plane[:, P * i : P * (i + 1)],
                 rhs=xt_codes[:].bitcast(FP8X4), rhs_scale=xt_plane[:], start=True, stop=True,
             )
-            nc.scalar.copy(u[i][:, :T], u_acc[i][:])
-
-        def pick_nbr(i):
-            nc.vector.tensor_copy(u_nbr[i][:], u[i][:].indirect(nbr[:]))
-            nc.scalar.activation(drive[i][:], u_nbr[i][:], ACT.Relu)
-            nc.scalar.activation(root[i][:], drive[i][:], ACT.Abs_reciprocal_sqrt, bias=1.0)
-            nc.scalar.activation(inv[i][:], root[i][:], ACT.Square)
+            nc.scalar.copy(new("u", i, U_WINDOW)[:, :T], acc[:])
 
         def make_z(i):
+            acc = psum.tile([P, T], F32, name="acc")
             nc.tensor.matmul_mx(
-                out=z_acc[i][:], lhsT=wa_codes[:, 2 * P * i : 2 * P * (i + 1)].bitcast(FP4X4),
+                out=acc[:], lhsT=wa_codes[:, 2 * P * i : 2 * P * (i + 1)].bitcast(FP4X4),
                 lhsT_scale=wa_plane[:, P * i : P * (i + 1)],
                 rhs=xt_codes[:].bitcast(FP8X4), rhs_scale=xt_plane[:], start=True, stop=True,
             )
-            nc.scalar.copy(z[i][:, :T], z_acc[i][:])
+            nc.scalar.copy(new("z", i, Z_WINDOW)[:, :T], acc[:])
+
+        def pick_nbr(i):
+            nc.vector.tensor_copy(new("u_nbr", i, J)[:], get("u", i)[:].indirect(nbr[:]))
+
+        def relu(i):
+            nc.scalar.activation(new("drive", i, J)[:], get("u_nbr", i)[:], ACT.Relu)
+
+        def root(i):
+            nc.scalar.activation(new("root", i, J)[:], get("drive", i)[:], ACT.Abs_reciprocal_sqrt, bias=1.0)
+
+        def square(i):
+            nc.scalar.activation(new("inv", i, J)[:], get("root", i)[:], ACT.Square)
 
         def pick_own(i):
-            nc.vector.tensor_copy(u_own[i][:], u[i][:].indirect(own[:]))
+            nc.vector.tensor_copy(new("u_own", i, J)[:], get("u", i)[:].indirect(own[:]))
+
+        def pick_z(i):
+            nc.vector.tensor_copy(new("z_own", i, J)[:], get("z", i)[:].indirect(own[:]))
 
         def divide(i):
-            nc.vector.tensor_tensor(quot[i][:], z[i][:].indirect(own[:]), inv[i][:], ALU.mult)
+            nc.gpsimd.tensor_tensor(new("quot", i, J)[:], get("z_own", i)[:], get("inv", i)[:], ALU.mult)
 
-        def finish(i):
-            nc.vector.scalar_tensor_tensor(res[i][:], u_own[i][:], share[:, i : i + 1], quot[i][:], ALU.mult, ALU.add)
-            nc.sync.dma_start(out[i * P : (i + 1) * P, :], res[i][:])
+        def scale(i):
+            nc.scalar.activation(new("part", i, J)[:], get("u_own", i)[:], ACT.Copy, scale=share[:, i : i + 1])
 
+        def finish_on_gpsimd(i):
+            nc.gpsimd.tensor_tensor(new("res", i, J)[:], get("quot", i)[:], get("part", i)[:], ALU.add)
+            nc.sync.dma_start(out[i * P : (i + 1) * P, :], get("res", i)[:])
+
+        def finish_on_vector(i, pieces):
+            res = new("res", i, J)
+            for h in pieces:
+                nc.vector.scalar_tensor_tensor(
+                    res[:, h], get("u_own", i)[:, h], share[:, i : i + 1], get("quot", i)[:, h], ALU.mult, ALU.add
+                )
+                nc.sync.dma_start(out[i * P : (i + 1) * P, h], res[:, h])
+
+        make_u(0)
         pick_nbr(0)
-        make_z(0)
+        make_u(1)
         pick_nbr(1)
+        make_z(0)
+        pick_z(0)
         make_z(1)
-        pick_own(0)
-        divide(0)
-        pick_nbr(2)
         make_z(2)
-        finish(0)
-        pick_own(1)
-        divide(1)
-        pick_nbr(3)
         make_z(3)
-        finish(1)
+        relu(0)
+        pick_own(0)
+        root(0)
+        make_u(2)
+        pick_nbr(2)
+        square(0)
+        pick_z(1)
+        divide(0)
+        relu(1)
+        scale(0)
+        pick_own(1)
+        finish_on_gpsimd(0)
+        root(1)
+        make_u(3)
+        pick_nbr(3)
+        square(1)
+        pick_z(2)
+        divide(1)
+        relu(2)
+        pick_z(3)
+        root(2)
+        scale(1)
         pick_own(2)
+        finish_on_gpsimd(1)
+        relu(3)
+        square(2)
         divide(2)
         pick_own(3)
-        finish(2)
+        root(3)
+        square(3)
         divide(3)
-        finish(3)
+        finish_on_vector(2, [slice(0, J)])
+        finish_on_vector(3, [slice(0, J // 2), slice(J // 2, J)])

from contextlib import ExitStack

import concourse.mybir as mybir

K, T, J, N = 512, 512, 512, 512
FLOPS = 2 * 2 * K * T * N

F32 = mybir.dt.float32
BF16 = mybir.dt.bfloat16
I32 = mybir.dt.int32
U32 = mybir.dt.uint32
U16 = mybir.dt.uint16
U8 = mybir.dt.uint8
FP8X4 = mybir.dt.float8_e4m3fn_x4
FP4X4 = mybir.dt.float4_e2m1fn_x4
ACT = mybir.ActivationFunctionType
ALU = mybir.AluOpType

P = 128
PACK = 4
TILES = N // P
U_WINDOW = 704
Z_WINDOW = 704


def tile_list_divided_by_neighbour_kernel(tc, xt_words, xt_scales, wa_words, wa_scales, wb, sh, offs, offs2, out):
    nc = tc.nc
    with ExitStack() as ctx:
        keep = ctx.enter_context(tc.tile_pool(name="keep", bufs=1))
        psum = ctx.enter_context(tc.psum_pool(name="psum", bufs=8))

        own = keep.tile([P, J // 16], U16, name="own")
        nbr = keep.tile([P, J // 16], U16, name="nbr")
        xt_codes = keep.tile([P, T], U32, name="xt_codes", align_bytes=64)
        xt_plane = keep.tile([P, T], U8, name="xt_plane", align_bytes=64)
        wa_codes = keep.tile([P, 2 * N], U8, name="wa_codes", align_bytes=64)
        wa_plane = keep.tile([P, N], U8, name="wa_plane", align_bytes=64)
        share = keep.tile([P, TILES], F32, name="share")
        warm = keep.tile([P, 1], F32, name="warm")
        warm_out = keep.tile([P, 1], F32, name="warm_out")

        chunks = [slice(0, P), slice(P, 2 * P), slice(2 * P, 4 * P)]
        wb_raw = [keep.tile([P, PACK, c.stop - c.start], F32, name="wb_raw%d" % c.start, tag="f" if c.start == 2 * P else "wb_raw%d" % c.start, align_bytes=64) for c in chunks]
        wb_grouped = [
            keep.tile([P, P, PACK], BF16, name="wb_grouped%d" % i, tag="h" if i == 3 else "wb_grouped%d" % i, align_bytes=64)
            for i in range(TILES)
        ]
        wb_codes = keep.tile([P, N], U32, name="wb_codes", align_bytes=64)
        wb_plane = keep.tile([P, N], U8, name="wb_plane", align_bytes=64)
        shared = {
            "u_nbr0": "a", "u_own0": "a", "u_own1": "a", "u_own2": "a",
            "root0": "b", "z_own1": "b", "z_own3": "b", "root1": "c", "z_own2": "c",
            "u_nbr2": "d", "part1": "d", "u_nbr3": "e", "u_own3": "e",
            "drive0": "f", "drive1": "f", "drive2": "f", "drive3": "f",
            "u_nbr1": "g", "part0": "g", "z_own0": "h",
        }
        made = {}

        def new(name, i, width):
            key = "%s%d" % (name, i)
            made[key] = keep.tile([P, width], F32, name=key, tag=shared.get(key, key), align_bytes=64)
            return made[key]

        def get(name, i):
            return made["%s%d" % (name, i)]

        nc.gpsimd.memset(warm[:], 1.0)
        nc.scalar.activation(warm_out[:], warm[:], ACT.Abs_reciprocal_sqrt)

        def load_wb(i):
            nc.sync.dma_start(wb_raw[i][:], wb[:, chunks[i]].rearrange("(p t) n -> p t n", t=PACK))

        def load_plane(plane, rows):
            for q in range(4):
                nc.sync.dma_start(plane[32 * q : 32 * q + 4, :].bitcast(I32), rows[0, 4 * q : 4 * q + 4, :].bitcast(I32))

        load_wb(0)
        load_plane(xt_plane, xt_scales)
        nc.sync.dma_start(xt_codes[:].bitcast(I32), xt_words[0].rearrange("p c r -> p (c r)").bitcast(I32))
        load_wb(1)
        nc.sync.dma_start(nbr[:], offs2)
        nc.sync.dma_start(wa_codes[:].bitcast(I32), wa_words[0].bitcast(I32))
        load_plane(wa_plane, wa_scales)
        load_wb(2)
        nc.sync.dma_start(own[:], offs)
        with nc.allow_non_contiguous_dma(reason="one share to a partition"):
            nc.sync.dma_start(share[:], sh.rearrange("(i p) o -> p (i o)", p=P))

        sources = [wb_raw[0][:], wb_raw[1][:], wb_raw[2][:, :, :P], wb_raw[2][:, :, P:]]
        for i in range(TILES):
            src = sources[i].rearrange("p t n -> p n t")
            cols = slice(i * P, (i + 1) * P)
            if i >= 2:
                nc.gpsimd.tensor_scalar(wb_grouped[i][:], src, 1.0, 0.0, ALU.mult, ALU.add)
            else:
                nc.vector.tensor_copy(wb_grouped[i][:], src)
            nc.vector.quantize_mx(
                out=wb_codes[:, cols].bitcast(FP8X4), scales=wb_plane[:, cols], in_=wb_grouped[i][:].rearrange("p n t -> p (n t)")
            )

        def make_u(i):
            acc = psum.tile([P, T], F32, name="acc")
            nc.tensor.matmul_mx(
                out=acc[:], lhsT=wb_codes[:, P * i : P * (i + 1)].bitcast(FP8X4), lhsT_scale=wb_plane[:, P * i : P * (i + 1)],
                rhs=xt_codes[:].bitcast(FP8X4), rhs_scale=xt_plane[:], start=True, stop=True,
            )
            nc.scalar.copy(new("u", i, U_WINDOW)[:, :T], acc[:])

        def make_z(i):
            acc = psum.tile([P, T], F32, name="acc")
            nc.tensor.matmul_mx(
                out=acc[:], lhsT=wa_codes[:, 2 * P * i : 2 * P * (i + 1)].bitcast(FP4X4),
                lhsT_scale=wa_plane[:, P * i : P * (i + 1)],
                rhs=xt_codes[:].bitcast(FP8X4), rhs_scale=xt_plane[:], start=True, stop=True,
            )
            nc.scalar.copy(new("z", i, Z_WINDOW)[:, :T], acc[:])

        def pick_nbr(i):
            nc.vector.tensor_copy(new("u_nbr", i, J)[:], get("u", i)[:].indirect(nbr[:]))

        def relu(i):
            nc.scalar.activation(new("drive", i, J)[:], get("u_nbr", i)[:], ACT.Relu)

        def root(i):
            nc.scalar.activation(new("root", i, J)[:], get("drive", i)[:], ACT.Abs_reciprocal_sqrt, bias=1.0)

        def square(i):
            nc.scalar.activation(new("inv", i, J)[:], get("root", i)[:], ACT.Square)

        def pick_own(i):
            nc.vector.tensor_copy(new("u_own", i, J)[:], get("u", i)[:].indirect(own[:]))

        def pick_z(i):
            nc.vector.tensor_copy(new("z_own", i, J)[:], get("z", i)[:].indirect(own[:]))

        def divide(i):
            nc.gpsimd.tensor_tensor(new("quot", i, J)[:], get("z_own", i)[:], get("inv", i)[:], ALU.mult)

        def scale(i):
            nc.scalar.activation(new("part", i, J)[:], get("u_own", i)[:], ACT.Copy, scale=share[:, i : i + 1])

        def finish_on_gpsimd(i):
            nc.gpsimd.tensor_tensor(new("res", i, J)[:], get("quot", i)[:], get("part", i)[:], ALU.add)
            nc.sync.dma_start(out[i * P : (i + 1) * P, :], get("res", i)[:])

        def finish_on_vector(i, pieces):
            res = new("res", i, J)
            for h in pieces:
                nc.vector.scalar_tensor_tensor(
                    res[:, h], get("u_own", i)[:, h], share[:, i : i + 1], get("quot", i)[:, h], ALU.mult, ALU.add
                )
                nc.sync.dma_start(out[i * P : (i + 1) * P, h], res[:, h])

        make_u(0)
        pick_nbr(0)
        make_u(1)
        pick_nbr(1)
        make_z(0)
        pick_z(0)
        make_z(1)
        make_z(2)
        make_z(3)
        relu(0)
        pick_own(0)
        root(0)
        make_u(2)
        pick_nbr(2)
        square(0)
        pick_z(1)
        divide(0)
        relu(1)
        scale(0)
        pick_own(1)
        finish_on_gpsimd(0)
        root(1)
        make_u(3)
        pick_nbr(3)
        square(1)
        pick_z(2)
        divide(1)
        relu(2)
        pick_z(3)
        root(2)
        scale(1)
        pick_own(2)
        finish_on_gpsimd(1)
        relu(3)
        square(2)
        divide(2)
        pick_own(3)
        root(3)
        square(3)
        divide(3)
        finish_on_vector(2, [slice(0, J)])
        finish_on_vector(3, [slice(0, J // 2), slice(J // 2, J)])
